import numpy as np
import ml_dtypes


def mxq(x, axis, fmt="e4m3"):
    dtype, down = {"e4m3": (ml_dtypes.float8_e4m3fn, 7), "e5m2": (ml_dtypes.float8_e5m2, 14)}[fmt]
    v = np.moveaxis(np.asarray(x, np.float32).astype(ml_dtypes.bfloat16).astype(np.float64), axis, -1)
    blocks = v.reshape(v.shape[:-1] + (-1, 32))
    amax = np.abs(blocks).max(-1, keepdims=True)
    byte = np.maximum(np.where(amax > 0, np.frexp(amax)[1] - 1 + 127, 0) - down, 1)
    scale = np.exp2(byte - 127.0)
    codes = (blocks / scale).astype(np.float32).astype(dtype).astype(np.float64)
    return np.moveaxis((codes * scale).reshape(v.shape), -1, axis)


WIDE = False


def mx_kscale(k):
    if not WIDE:
        return np.ones(k)
    levels = np.array([10, -10, 5, -5, 0])
    if k % 512:
        return np.exp2(np.random.permutation(np.resize(levels, k // 32))).repeat(32)
    a = np.empty((k // 512, 16))
    for p in range(k // 512):
        a[p, :8] = np.random.permutation(np.resize(levels, 8))
        for g in range(8):
            far = levels[np.abs(levels - a[p, g]) >= 10]
            a[p, g + 8] = far[np.random.randint(len(far))]
    return np.exp2(a.ravel()).repeat(32)


def f64(x):
    return np.asarray(x).astype(np.float64)


def striped(idx):
    return np.tile(idx.reshape(-1, 16).T, (8, 1)).astype(np.uint16)


def unstriped(offs):
    return offs[:16].T.reshape(-1).astype(np.int64)


def pack_weight(w):
    k, n = w.shape
    w = f64(np.asarray(w, np.float32).astype(ml_dtypes.bfloat16)).reshape(k // 32, 32, n)
    amax = np.abs(w).max(1)
    byte = np.clip(np.where(amax > 0, np.frexp(amax)[1] - 1 + 127 - 7, 1), 1, 254)
    scaled = (w * np.exp2(127.0 - byte)[:, None, :]).reshape(k, n).astype(np.float32)
    words = np.ascontiguousarray(scaled.reshape(k // 512, 128, 4, n).transpose(0, 1, 3, 2)).astype(ml_dtypes.float8_e4m3fn).view(np.uint8)
    return words, np.ascontiguousarray(byte.astype(np.uint8).reshape(k // 512, 16, n))


def unpack_weight(words, scales):
    g, p, n, _ = words.shape
    vals = np.ascontiguousarray(words).view(ml_dtypes.float8_e4m3fn).astype(np.float64) * np.repeat(np.exp2(scales.astype(np.float64) - 127.0), 8, axis=1)[..., None]
    return vals.transpose(0, 1, 3, 2).reshape(g * 512, n)


def relu(v):
    return np.maximum(v, 0.0)


K, T, D, S, V, N = 512, 512, 3, 768, 256, 512
P = 2 ** 7


def setup_inputs():
    n = np.random.standard_normal
    s = mx_kscale(K)[:, None]
    words, scales = pack_weight(n((K, N)) / np.sqrt(K) / s)
    return {
        "xT": (n((K, T)) * s / np.sqrt(D)).astype(ml_dtypes.bfloat16).astype(np.float32),
        "w_words": words,
        "w_scales": scales,
        "b": (0.3 * n((N, 1))).astype(np.float32),
        "gate": np.tile(np.random.uniform(0.5, 1.5, (D, 1, V)), (1, P, 1)).astype(ml_dtypes.bfloat16).astype(np.float32),
        "offs": striped(np.concatenate([np.random.permutation(T)[:V] for _ in range(D)])),
    }


def reference(xT, w_words, w_scales, b, gate, offs):
    w = unpack_weight(w_words, w_scales)
    idx = unstriped(offs)
    x = sum(f64(gate)[d, :1] * f64(xT)[:, idx[d * V:(d + 1) * V]] for d in range(D))
    return relu((w.T @ mxq(x, 0, "e4m3")) + f64(b))

@@ -1,0 +1,194 @@
+from contextlib import ExitStack
+
+import concourse.mybir as mybir
+from concourse.masks import make_identity
+
+K, T, D, V, N = 512, 512, 3, 256, 512
+FLOPS = 2 * K * V * N
+
+F32 = mybir.dt.float32
+BF16 = mybir.dt.bfloat16
+U32 = mybir.dt.uint32
+I32 = mybir.dt.int32
+U16 = mybir.dt.uint16
+U8 = mybir.dt.uint8
+FP8X4 = mybir.dt.float8_e4m3fn_x4
+MULT = mybir.AluOpType.mult
+ADD = mybir.AluOpType.add
+MAX = mybir.AluOpType.max
+COPY = mybir.ActivationFunctionType.Copy
+RELU = mybir.ActivationFunctionType.Relu
+
+P = 128
+HALF = 128
+LIST_COL = 16
+GATE_ROW_STEP = 127
+GATE_COL = (0, 2, 3)
+BIAS_COL = 4
+
+
+def tile_picked_bag_lin_relu_sub_l_kernel(tc, xT, w_words, w_scales, b, gate, offs, out):
+    nc = tc.nc
+    with ExitStack() as ctx:
+        sb = ctx.enter_context(tc.tile_pool(name="sb", bufs=1))
+        ps = ctx.enter_context(tc.psum_pool(name="ps", bufs=1))
+
+        offsets = sb.tile([P, D * V // LIST_COL], U16, name="offsets")
+        rows = sb.tile([P, V], F32, name="rows")
+        nc.vector.memset(rows[:], 0.0)
+        warm = sb.tile([P, 1], F32, name="warm")
+        zero = sb.tile([P, 1], F32, name="zero")
+        nc.gpsimd.memset(zero[:], 0.0)
+        nc.scalar.activation(out=warm[:], in_=zero[:], func=RELU)
+        ident = sb.tile([P, P], F32, name="ident")
+        make_identity(nc, ident[:])
+        w_plane = sb.tile([P, N], U8, name="w_plane", align_bytes=64)
+        nc.gpsimd.memset(w_plane[:].bitcast(I32), 0)
+
+        x_view = xT.rearrange("(p u e) c -> p u e c", u=2, e=2)
+        raw = {}
+
+        def load_x(u, c):
+            raw[u, c] = sb.tile([P, 2, T // 2], F32, name=f"raw{u}{c}")
+            nc.sync.dma_start(out=raw[u, c][:], in_=x_view[:, u, :, c * (T // 2) : (c + 1) * (T // 2)])
+
+        load_x(0, 0)
+        load_x(0, 1)
+        nc.sync.dma_start(offsets[:], offs)
+        nc.sync.dma_start(out=rows[0:4, :], in_=gate.rearrange("d p v -> (d p) v")[0 : D * P : GATE_ROW_STEP, :])
+        nc.sync.dma_start(out=rows[4:6, :], in_=b.rearrange("(r c) o -> r (c o)", r=2))
+        load_x(1, 0)
+        load_x(1, 1)
+        w_codes = sb.tile([P, N], I32, name="w_codes", align_bytes=64)
+        nc.sync.dma_start(out=w_codes[:], in_=w_words[0].rearrange("p n t -> p (n t)").bitcast(I32))
+        for q in range(4):
+            nc.sync.dma_start(
+                out=w_plane[32 * q : 32 * q + 4, :].bitcast(I32), in_=w_scales[0, 4 * q : 4 * q + 4, :].bitcast(I32)
+            )
+
+        window = [sb.tile([P, T, 2], BF16, name=f"window{u}") for u in range(2)]
+        for c in range(2):
+            nc.vector.tensor_copy(
+                out=window[0][:, c * (T // 2) : (c + 1) * (T // 2), :], in_=raw[0, c][:].rearrange("p e c -> p c e")
+            )
+
+        cols_ps = ps.tile([P, 2, P], F32, name="cols_ps", tag="tail0")
+        for h in range(2):
+            nc.tensor.transpose(cols_ps[:, h, :], rows[:, h * HALF : (h + 1) * HALF], ident[:])
+        cols = sb.tile([P, 2, 8], F32, name="cols")
+        nc.scalar.copy(out=cols[:], in_=cols_ps[:, :, 0:8])
+
+        for c in range(2):
+            nc.scalar.copy(
+                out=window[1][:, c * (T // 2) : (c + 1) * (T // 2), :], in_=raw[1, c][:].rearrange("p e c -> p c e")
+            )
+
+        first_ps = [ps.tile([P, 2, P], F32, name=f"first_ps{u}", tag=f"first{u}") for u in range(2)]
+        rest_ps = {
+            (u, h): ps.tile([P, 2, P], F32, name=f"rest_ps{u}{h}", tag=f"rest{u}{h}") for u in range(2) for h in range(2)
+        }
+        part = {}
+        x_rows = [sb.tile([P, 2, 2 * P], BF16, name=f"x_rows{h}") for h in range(2)]
+
+        def turned(u, h, d):
+            return first_ps[u][:, h, :] if d == 0 else rest_ps[u, h][:, d - 1, :]
+
+        def weight(h, d):
+            return cols[:, h, GATE_COL[d] : GATE_COL[d] + 1]
+
+        def gather(u, d, halves):
+            n = HALF * len(halves)
+            start = (d * V + halves[0] * HALF) // LIST_COL
+            picked = sb.tile([P, 2 * n], BF16, name=f"picked{u}{d}{halves[0]}")
+            nc.vector.tensor_copy(
+                out=picked[:].bitcast(U32),
+                in_=window[u][:].rearrange("p c e -> p (c e)").bitcast(U32).indirect(offsets[:, start : start + n // LIST_COL]),
+            )
+            for i, h in enumerate(halves):
+                nc.tensor.transpose(turned(u, h, d), picked[:].bitcast(F32)[:, i * HALF : (i + 1) * HALF], ident[:])
+            if d == 0:
+                for h in halves:
+                    part[u, h, 0] = sb.tile([P, 2 * P], F32, name=f"part{u}{h}0")
+                    nc.scalar.activation(out=part[u, h, 0][:], in_=turned(u, h, 0).bitcast(BF16), func=COPY, scale=weight(h, 0))
+
+        def add_term(u, h, d):
+            if d == 1:
+                part[u, h, 1] = sb.tile([P, 2 * P], F32, name=f"part{u}{h}1")
+                dst = part[u, h, 1][:]
+            else:
+                dst = x_rows[h][:, u, :]
+            nc.vector.scalar_tensor_tensor(
+                out=dst, in0=turned(u, h, d).bitcast(BF16), scalar=weight(h, d), in1=part[u, h, d - 1][:], op0=MULT, op1=ADD
+            )
+
+        back_ps = {}
+        grouped = {}
+
+        def turn_back(u, h):
+            if u == 0:
+                back_ps[h] = ps.tile([P, 2, P], F32, name=f"back_ps{h}", tag=f"tail{h}")
+            nc.tensor.transpose(back_ps[h][:, u, :], x_rows[h][:, u, :].bitcast(F32), ident[:])
+            if u == 1:
+                grouped[h] = sb.tile([P, 4 * HALF], BF16, name=f"grouped{h}", align_bytes=64)
+                nc.scalar.copy(
+                    out=grouped[h][:].bitcast(F32).rearrange("p (v u) -> p v u", u=2),
+                    in_=back_ps[h][:].rearrange("p u v -> p v u"),
+                )
+
+        acc = {}
+
+        def product(h):
+            codes = sb.tile([P, HALF], U32, name=f"codes{h}", align_bytes=64)
+            plane = sb.tile([P, HALF], U8, name=f"plane{h}", align_bytes=64)
+            nc.vector.quantize_mx(out=codes[:].bitcast(FP8X4), scales=plane[:], in_=grouped[h][:])
+            for g in range(2):
+                acc[h, g] = ps.tile([P, 2, HALF], F32, name=f"acc{h}{g}", tag=(f"tail{h}", f"first{h}")[g])
+                for i in range(2):
+                    m = slice((2 * g + i) * P, (2 * g + i + 1) * P)
+                    nc.tensor.matmul_mx(
+                        out=acc[h, g][:, i, :],
+                        lhsT=w_codes[:, m].bitcast(FP8X4),
+                        lhsT_scale=w_plane[:, m],
+                        rhs=codes[:].bitcast(FP8X4),
+                        rhs_scale=plane[:],
+                        start=True,
+                        stop=True,
+                    )
+
+        out_view = out.rearrange("(j p) v -> p j v", p=P)
+
+        def finish(h, g):
+            res = sb.tile([P, 2, HALF], F32, name=f"res{h}{g}")
+            for i in range(2):
+                bias = cols[:, i, BIAS_COL + g : BIAS_COL + g + 1]
+                if g == 0:
+                    nc.vector.tensor_scalar(out=res[:, i, :], in0=acc[h, g][:, i, :], scalar1=bias, scalar2=0.0, op0=ADD, op1=MAX)
+                else:
+                    nc.scalar.activation(out=res[:, i, :], in_=acc[h, g][:, i, :], func=RELU, bias=bias)
+            nc.sync.dma_start(out=out_view[:, 2 * g : 2 * g + 2, h * HALF : (h + 1) * HALF], in_=res[:])
+
+        for d in range(D):
+            gather(0, d, (0, 1))
+        for d in range(D):
+            gather(1, d, (0,))
+        gather(1, 0, (1,))
+        gather(1, 1, (1,))
+        add_term(0, 0, 1)
+        gather(1, 2, (1,))
+        add_term(1, 0, 1)
+        add_term(0, 0, 2)
+        turn_back(0, 0)
+        add_term(0, 1, 1)
+        add_term(1, 0, 2)
+        turn_back(1, 0)
+        add_term(1, 1, 1)
+        add_term(0, 1, 2)
+        turn_back(0, 1)
+        add_term(1, 1, 2)
+        turn_back(1, 1)
+        product(0)
+        finish(0, 0)
+        finish(0, 1)
+        product(1)
+        finish(1, 0)
+        finish(1, 1)

@@ -25,6 +25,8 @@ LIST_COL = 16
 GATE_ROW_STEP = 127
 GATE_COL = (0, 2, 3)
 BIAS_COL = 4
+CUTS = ((0, 320, T), (0, 256, T))
+SCALAR_SHARE = 64
 
 
 def tile_picked_bag_lin_relu_sub_l_kernel(tc, xT, w_words, w_scales, b, gate, offs, out):
@@ -49,8 +51,9 @@ def tile_picked_bag_lin_relu_sub_l_kernel(tc, xT, w_words, w_scales, b, gate, of
         raw = {}
 
         def load_x(u, c):
-            raw[u, c] = sb.tile([P, 2, T // 2], F32, name=f"raw{u}{c}")
-            nc.sync.dma_start(out=raw[u, c][:], in_=x_view[:, u, :, c * (T // 2) : (c + 1) * (T // 2)])
+            lo, hi = CUTS[u][c], CUTS[u][c + 1]
+            raw[u, c] = sb.tile([P, 2, hi - lo], F32, name=f"raw{u}{c}")
+            nc.sync.dma_start(out=raw[u, c][:], in_=x_view[:, u, :, lo:hi])
 
         load_x(0, 0)
         load_x(0, 1)
@@ -67,36 +70,42 @@ def tile_picked_bag_lin_relu_sub_l_kernel(tc, xT, w_words, w_scales, b, gate, of
             )
 
         window = [sb.tile([P, T, 2], BF16, name=f"window{u}") for u in range(2)]
-        for c in range(2):
-            nc.vector.tensor_copy(
-                out=window[0][:, c * (T // 2) : (c + 1) * (T // 2), :], in_=raw[0, c][:].rearrange("p e c -> p c e")
-            )
 
-        cols_ps = ps.tile([P, 2, P], F32, name="cols_ps", tag="tail0")
+        def pair_up(copy, u, c, lo, hi):
+            base = CUTS[u][c]
+            copy(out=window[u][:, lo:hi, :], in_=raw[u, c][:, :, lo - base : hi - base].rearrange("p e c -> p c e"))
+
+        pair_up(nc.vector.tensor_copy, 0, 0, 0, CUTS[0][1])
+        pair_up(nc.vector.tensor_copy, 0, 1, CUTS[0][1], T - SCALAR_SHARE)
+        pair_up(nc.scalar.copy, 0, 1, T - SCALAR_SHARE, T)
+
+        def bank(i, slots, name):
+            return ps.tile([P, slots, P], F32, name=name, tag=f"bank{i}")
+
+        cols_ps = bank(0, 2, "cols_ps")
         for h in range(2):
             nc.tensor.transpose(cols_ps[:, h, :], rows[:, h * HALF : (h + 1) * HALF], ident[:])
         cols = sb.tile([P, 2, 8], F32, name="cols")
         nc.scalar.copy(out=cols[:], in_=cols_ps[:, :, 0:8])
 
-        for c in range(2):
-            nc.scalar.copy(
-                out=window[1][:, c * (T // 2) : (c + 1) * (T // 2), :], in_=raw[1, c][:].rearrange("p e c -> p c e")
-            )
+        def gpsimd_copy(out, in_):
+            nc.gpsimd.tensor_scalar(out=out, in0=in_, scalar1=1.0, scalar2=0.0, op0=MULT, op1=ADD)
 
-        first_ps = [ps.tile([P, 2, P], F32, name=f"first_ps{u}", tag=f"first{u}") for u in range(2)]
-        rest_ps = {
-            (u, h): ps.tile([P, 2, P], F32, name=f"rest_ps{u}{h}", tag=f"rest{u}{h}") for u in range(2) for h in range(2)
-        }
-        part = {}
-        x_rows = [sb.tile([P, 2, 2 * P], BF16, name=f"x_rows{h}") for h in range(2)]
+        pair_up(gpsimd_copy, 1, 0, CUTS[1][0], CUTS[1][1])
+        pair_up(nc.scalar.copy, 1, 1, CUTS[1][1], CUTS[1][2])
 
-        def turned(u, h, d):
-            return first_ps[u][:, h, :] if d == 0 else rest_ps[u, h][:, d - 1, :]
+        turned = {}
+
+        def place(i, u, d, halves):
+            tile = bank(i, len(halves), f"turned{u}{d}{halves[0]}")
+            for slot, h in enumerate(halves):
+                turned[u, h, d] = tile[:, slot, :]
 
         def weight(h, d):
             return cols[:, h, GATE_COL[d] : GATE_COL[d] + 1]
 
-        def gather(u, d, halves):
+        def gather(u, d, halves, bank_no):
+            place(bank_no, u, d, halves)
             n = HALF * len(halves)
             start = (d * V + halves[0] * HALF) // LIST_COL
             picked = sb.tile([P, 2 * n], BF16, name=f"picked{u}{d}{halves[0]}")
@@ -105,31 +114,37 @@ def tile_picked_bag_lin_relu_sub_l_kernel(tc, xT, w_words, w_scales, b, gate, of
                 in_=window[u][:].rearrange("p c e -> p (c e)").bitcast(U32).indirect(offsets[:, start : start + n // LIST_COL]),
             )
             for i, h in enumerate(halves):
-                nc.tensor.transpose(turned(u, h, d), picked[:].bitcast(F32)[:, i * HALF : (i + 1) * HALF], ident[:])
-            if d == 0:
-                for h in halves:
-                    part[u, h, 0] = sb.tile([P, 2 * P], F32, name=f"part{u}{h}0")
-                    nc.scalar.activation(out=part[u, h, 0][:], in_=turned(u, h, 0).bitcast(BF16), func=COPY, scale=weight(h, 0))
+                nc.tensor.transpose(turned[u, h, d], picked[:].bitcast(F32)[:, i * HALF : (i + 1) * HALF], ident[:])
 
-        def add_term(u, h, d):
-            if d == 1:
-                part[u, h, 1] = sb.tile([P, 2 * P], F32, name=f"part{u}{h}1")
-                dst = part[u, h, 1][:]
-            else:
-                dst = x_rows[h][:, u, :]
+        grouped = [sb.tile([P, 4 * HALF], BF16, name=f"grouped{h}", align_bytes=64) for h in range(2)]
+
+        term = {}
+        part = {}
+        x_rows = [sb.tile([P, 2, 2 * P], BF16, name=f"x_rows{h}") for h in range(2)]
+        back_ps = {}
+
+        def weigh(u, h, d):
+            term[u, h, d] = sb.tile([P, 2 * P], F32, name=f"term{u}{h}{d}")
+            nc.scalar.activation(out=term[u, h, d][:], in_=turned[u, h, d].bitcast(BF16), func=COPY, scale=weight(h, d))
+
+        def add_two(u, h):
+            part[u, h] = sb.tile([P, 2 * P], F32, name=f"part{u}{h}")
+            nc.gpsimd.tensor_tensor(out=part[u, h][:], in0=term[u, h, 0][:], in1=term[u, h, 1][:], op=ADD)
+
+        def add_second(u, h):
+            part[u, h] = sb.tile([P, 2 * P], F32, name=f"part{u}{h}")
             nc.vector.scalar_tensor_tensor(
-                out=dst, in0=turned(u, h, d).bitcast(BF16), scalar=weight(h, d), in1=part[u, h, d - 1][:], op0=MULT, op1=ADD
+                out=part[u, h][:], in0=turned[u, h, 1].bitcast(BF16), scalar=weight(h, 1), in1=term[u, h, 0][:], op0=MULT, op1=ADD
             )
 
-        back_ps = {}
-        grouped = {}
-
-        def turn_back(u, h):
+        def add_last(u, h):
+            nc.vector.scalar_tensor_tensor(
+                out=x_rows[h][:, u, :], in0=turned[u, h, 2].bitcast(BF16), scalar=weight(h, 2), in1=part[u, h][:], op0=MULT, op1=ADD
+            )
             if u == 0:
-                back_ps[h] = ps.tile([P, 2, P], F32, name=f"back_ps{h}", tag=f"tail{h}")
+                back_ps[h] = bank((7, 4)[h], 2, f"back_ps{h}")
             nc.tensor.transpose(back_ps[h][:, u, :], x_rows[h][:, u, :].bitcast(F32), ident[:])
             if u == 1:
-                grouped[h] = sb.tile([P, 4 * HALF], BF16, name=f"grouped{h}", align_bytes=64)
                 nc.scalar.copy(
                     out=grouped[h][:].bitcast(F32).rearrange("p (v u) -> p v u", u=2),
                     in_=back_ps[h][:].rearrange("p u v -> p v u"),
@@ -137,58 +152,59 @@ def tile_picked_bag_lin_relu_sub_l_kernel(tc, xT, w_words, w_scales, b, gate, of
 
         acc = {}
 
-        def product(h):
+        def product(h, banks):
             codes = sb.tile([P, HALF], U32, name=f"codes{h}", align_bytes=64)
             plane = sb.tile([P, HALF], U8, name=f"plane{h}", align_bytes=64)
             nc.vector.quantize_mx(out=codes[:].bitcast(FP8X4), scales=plane[:], in_=grouped[h][:])
-            for g in range(2):
-                acc[h, g] = ps.tile([P, 2, HALF], F32, name=f"acc{h}{g}", tag=(f"tail{h}", f"first{h}")[g])
-                for i in range(2):
-                    m = slice((2 * g + i) * P, (2 * g + i + 1) * P)
-                    nc.tensor.matmul_mx(
-                        out=acc[h, g][:, i, :],
-                        lhsT=w_codes[:, m].bitcast(FP8X4),
-                        lhsT_scale=w_plane[:, m],
-                        rhs=codes[:].bitcast(FP8X4),
-                        rhs_scale=plane[:],
-                        start=True,
-                        stop=True,
-                    )
+            per_bank = 4 // len(banks)
+            tiles = [bank(i, per_bank, f"acc{h}{i}") for i in banks]
+            for j in range(4):
+                acc[h, j] = tiles[j // per_bank][:, j % per_bank, :]
+                m = slice(j * P, (j + 1) * P)
+                nc.tensor.matmul_mx(
+                    out=acc[h, j],
+                    lhsT=w_codes[:, m].bitcast(FP8X4),
+                    lhsT_scale=w_plane[:, m],
+                    rhs=codes[:].bitcast(FP8X4),
+                    rhs_scale=plane[:],
+                    start=True,
+                    stop=True,
+                )
 
         out_view = out.rearrange("(j p) v -> p j v", p=P)
 
-        def finish(h, g):
-            res = sb.tile([P, 2, HALF], F32, name=f"res{h}{g}")
-            for i in range(2):
-                bias = cols[:, i, BIAS_COL + g : BIAS_COL + g + 1]
-                if g == 0:
-                    nc.vector.tensor_scalar(out=res[:, i, :], in0=acc[h, g][:, i, :], scalar1=bias, scalar2=0.0, op0=ADD, op1=MAX)
+        def finish(h, js, on_vector):
+            res = sb.tile([P, len(js), HALF], F32, name=f"res{h}{js[0]}")
+            for i, j in enumerate(js):
+                bias = cols[:, j % 2, BIAS_COL + j // 2 : BIAS_COL + j // 2 + 1]
+                if on_vector[i]:
+                    nc.vector.tensor_scalar(out=res[:, i, :], in0=acc[h, j], scalar1=bias, scalar2=0.0, op0=ADD, op1=MAX)
                 else:
-                    nc.scalar.activation(out=res[:, i, :], in_=acc[h, g][:, i, :], func=RELU, bias=bias)
-            nc.sync.dma_start(out=out_view[:, 2 * g : 2 * g + 2, h * HALF : (h + 1) * HALF], in_=res[:])
+                    nc.scalar.activation(out=res[:, i, :], in_=acc[h, j], func=RELU, bias=bias)
+            nc.sync.dma_start(out=out_view[:, js[0] : js[-1] + 1, h * HALF : (h + 1) * HALF], in_=res[:])
 
         for d in range(D):
-            gather(0, d, (0, 1))
-        for d in range(D):
-            gather(1, d, (0,))
-        gather(1, 0, (1,))
-        gather(1, 1, (1,))
-        add_term(0, 0, 1)
-        gather(1, 2, (1,))
-        add_term(1, 0, 1)
-        add_term(0, 0, 2)
-        turn_back(0, 0)
-        add_term(0, 1, 1)
-        add_term(1, 0, 2)
-        turn_back(1, 0)
-        add_term(1, 1, 1)
-        add_term(0, 1, 2)
-        turn_back(0, 1)
-        add_term(1, 1, 2)
-        turn_back(1, 1)
-        product(0)
-        finish(0, 0)
-        finish(0, 1)
-        product(1)
-        finish(1, 0)
-        finish(1, 1)
+            gather(0, d, (0, 1), 1 + d)
+        for h in range(2):
+            weigh(0, h, 0)
+            weigh(0, h, 1)
+            add_two(0, h)
+        for d, bank_no in enumerate((4, 0, 5)):
+            gather(1, d, (0,), bank_no)
+        weigh(1, 0, 0)
+        weigh(1, 0, 1)
+        add_two(1, 0)
+        for d, bank_no in enumerate((1, 2, 6)):
+            gather(1, d, (1,), bank_no)
+        weigh(1, 1, 0)
+        add_last(0, 0)
+        add_last(0, 1)
+        add_second(1, 1)
+        add_last(1, 0)
+        add_last(1, 1)
+        product(0, (0, 1))
+        product(1, (2, 3, 5, 6))
+        finish(0, (0, 1), (True, True))
+        finish(0, (2, 3), (False, False))
+        finish(1, (0, 1), (True, False))
+        finish(1, (2, 3), (True, False))

@@ -40,12 +40,12 @@ def tile_picked_bag_lin_relu_sub_l_kernel(tc, xT, w_words, w_scales, b, gate, of
         nc.vector.memset(rows[:], 0.0)
         warm = sb.tile([P, 1], F32, name="warm")
         zero = sb.tile([P, 1], F32, name="zero")
-        nc.gpsimd.memset(zero[:], 0.0)
+        nc.vector.memset(zero[:], 0.0)
         nc.scalar.activation(out=warm[:], in_=zero[:], func=RELU)
         ident = sb.tile([P, P], F32, name="ident")
         make_identity(nc, ident[:])
         w_plane = sb.tile([P, N], U8, name="w_plane", align_bytes=64)
-        nc.gpsimd.memset(w_plane[:].bitcast(I32), 0)
+        nc.vector.memset(w_plane[:].bitcast(I32), 0)
 
         x_view = xT.rearrange("(p u e) c -> p u e c", u=2, e=2)
         raw = {}
@@ -56,8 +56,8 @@ def tile_picked_bag_lin_relu_sub_l_kernel(tc, xT, w_words, w_scales, b, gate, of
             nc.sync.dma_start(out=raw[u, c][:], in_=x_view[:, u, :, lo:hi])
 
         load_x(0, 0)
-        load_x(0, 1)
         nc.sync.dma_start(offsets[:], offs)
+        load_x(0, 1)
         nc.sync.dma_start(out=rows[0:4, :], in_=gate.rearrange("d p v -> (d p) v")[0 : D * P : GATE_ROW_STEP, :])
         nc.sync.dma_start(out=rows[4:6, :], in_=b.rearrange("(r c) o -> r (c o)", r=2))
         load_x(1, 0)
@@ -104,8 +104,12 @@ def tile_picked_bag_lin_relu_sub_l_kernel(tc, xT, w_words, w_scales, b, gate, of
         def weight(h, d):
             return cols[:, h, GATE_COL[d] : GATE_COL[d] + 1]
 
-        def gather(u, d, halves, bank_no):
-            place(bank_no, u, d, halves)
+        def gather(u, d, halves, banks):
+            if len(banks) == 1:
+                place(banks[0], u, d, halves)
+            else:
+                for h in halves:
+                    place(banks[h], u, d, (h,))
             n = HALF * len(halves)
             start = (d * V + halves[0] * HALF) // LIST_COL
             picked = sb.tile([P, 2 * n], BF16, name=f"picked{u}{d}{halves[0]}")
@@ -142,13 +146,11 @@ def tile_picked_bag_lin_relu_sub_l_kernel(tc, xT, w_words, w_scales, b, gate, of
                 out=x_rows[h][:, u, :], in0=turned[u, h, 2].bitcast(BF16), scalar=weight(h, 2), in1=part[u, h][:], op0=MULT, op1=ADD
             )
             if u == 0:
-                back_ps[h] = bank((7, 4)[h], 2, f"back_ps{h}")
+                back_ps[h] = bank((6, 7)[h], 2, f"back_ps{h}")
             nc.tensor.transpose(back_ps[h][:, u, :], x_rows[h][:, u, :].bitcast(F32), ident[:])
-            if u == 1:
-                nc.scalar.copy(
-                    out=grouped[h][:].bitcast(F32).rearrange("p (v u) -> p v u", u=2),
-                    in_=back_ps[h][:].rearrange("p u v -> p v u"),
-                )
+
+        def interleave(h, copy):
+            copy(out=grouped[h][:].bitcast(F32).rearrange("p (v u) -> p v u", u=2), in_=back_ps[h][:].rearrange("p u v -> p v u"))
 
         acc = {}
 
@@ -183,28 +185,31 @@ def tile_picked_bag_lin_relu_sub_l_kernel(tc, xT, w_words, w_scales, b, gate, of
                     nc.scalar.activation(out=res[:, i, :], in_=acc[h, j], func=RELU, bias=bias)
             nc.sync.dma_start(out=out_view[:, js[0] : js[-1] + 1, h * HALF : (h + 1) * HALF], in_=res[:])
 
-        for d in range(D):
-            gather(0, d, (0, 1), 1 + d)
+        gather(0, 0, (0, 1), (1,))
+        gather(0, 1, (0, 1), (2,))
+        gather(0, 2, (0, 1), (3,))
         for h in range(2):
             weigh(0, h, 0)
             weigh(0, h, 1)
             add_two(0, h)
-        for d, bank_no in enumerate((4, 0, 5)):
-            gather(1, d, (0,), bank_no)
+        gather(1, 0, (0, 1), (4,))
+        gather(1, 1, (0,), (0,))
+        gather(1, 2, (0,), (2,))
+        gather(1, 1, (1,), (5,))
         weigh(1, 0, 0)
-        weigh(1, 0, 1)
-        add_two(1, 0)
-        for d, bank_no in enumerate((1, 2, 6)):
-            gather(1, d, (1,), bank_no)
         weigh(1, 1, 0)
+        add_second(1, 0)
         add_last(0, 0)
-        add_last(0, 1)
-        add_second(1, 1)
         add_last(1, 0)
+        gather(1, 2, (1,), (1,))
+        add_second(1, 1)
+        add_last(0, 1)
+        interleave(0, nc.scalar.copy)
         add_last(1, 1)
-        product(0, (0, 1))
-        product(1, (2, 3, 5, 6))
-        finish(0, (0, 1), (True, True))
-        finish(0, (2, 3), (False, False))
-        finish(1, (0, 1), (True, False))
-        finish(1, (2, 3), (True, False))
+        interleave(1, nc.scalar.copy)
+        product(0, (4, 0, 2, 6))
+        product(1, (1, 3, 5, 7))
+        finish(0, (0, 1), (True, False))
+        finish(0, (2, 3), (True, False))
+        finish(1, (0, 1), (False, True))
+        finish(1, (2, 3), (False, True))

@@ -25,8 +25,9 @@ LIST_COL = 16
 GATE_ROW_STEP = 127
 GATE_COL = (0, 2, 3)
 BIAS_COL = 4
-CUTS = ((0, 320, T), (0, 256, T))
-SCALAR_SHARE = 64
+CUTS = ((0, 256, T), (0, 256, T))
+SCALAR_SHARE = 80
+GPSIMD_SHARE = 112
 
 
 def tile_picked_bag_lin_relu_sub_l_kernel(tc, xT, w_words, w_scales, b, gate, offs, out):
@@ -56,8 +57,8 @@ def tile_picked_bag_lin_relu_sub_l_kernel(tc, xT, w_words, w_scales, b, gate, of
             nc.sync.dma_start(out=raw[u, c][:], in_=x_view[:, u, :, lo:hi])
 
         load_x(0, 0)
-        nc.sync.dma_start(offsets[:], offs)
         load_x(0, 1)
+        nc.sync.dma_start(offsets[:], offs)
         nc.sync.dma_start(out=rows[0:4, :], in_=gate.rearrange("d p v -> (d p) v")[0 : D * P : GATE_ROW_STEP, :])
         nc.sync.dma_start(out=rows[4:6, :], in_=b.rearrange("(r c) o -> r (c o)", r=2))
         load_x(1, 0)
@@ -91,8 +92,9 @@ def tile_picked_bag_lin_relu_sub_l_kernel(tc, xT, w_words, w_scales, b, gate, of
         def gpsimd_copy(out, in_):
             nc.gpsimd.tensor_scalar(out=out, in0=in_, scalar1=1.0, scalar2=0.0, op0=MULT, op1=ADD)
 
-        pair_up(gpsimd_copy, 1, 0, CUTS[1][0], CUTS[1][1])
-        pair_up(nc.scalar.copy, 1, 1, CUTS[1][1], CUTS[1][2])
+        pair_up(nc.scalar.copy, 1, 0, CUTS[1][0], CUTS[1][1])
+        pair_up(nc.scalar.copy, 1, 1, CUTS[1][1], T - GPSIMD_SHARE)
+        pair_up(gpsimd_copy, 1, 1, T - GPSIMD_SHARE, T)
 
         turned = {}
 

from contextlib import ExitStack

import concourse.mybir as mybir
from concourse.masks import make_identity

K, T, D, V, N = 512, 512, 3, 256, 512
FLOPS = 2 * K * V * N

F32 = mybir.dt.float32
BF16 = mybir.dt.bfloat16
U32 = mybir.dt.uint32
I32 = mybir.dt.int32
U16 = mybir.dt.uint16
U8 = mybir.dt.uint8
FP8X4 = mybir.dt.float8_e4m3fn_x4
MULT = mybir.AluOpType.mult
ADD = mybir.AluOpType.add
MAX = mybir.AluOpType.max
COPY = mybir.ActivationFunctionType.Copy
RELU = mybir.ActivationFunctionType.Relu

P = 128
HALF = 128
LIST_COL = 16
GATE_ROW_STEP = 127
GATE_COL = (0, 2, 3)
BIAS_COL = 4
CUTS = ((0, 256, T), (0, 256, T))
SCALAR_SHARE = 80
GPSIMD_SHARE = 112


def tile_picked_bag_lin_relu_sub_l_kernel(tc, xT, w_words, w_scales, b, gate, offs, out):
    nc = tc.nc
    with ExitStack() as ctx:
        sb = ctx.enter_context(tc.tile_pool(name="sb", bufs=1))
        ps = ctx.enter_context(tc.psum_pool(name="ps", bufs=1))

        offsets = sb.tile([P, D * V // LIST_COL], U16, name="offsets")
        rows = sb.tile([P, V], F32, name="rows")
        nc.vector.memset(rows[:], 0.0)
        warm = sb.tile([P, 1], F32, name="warm")
        zero = sb.tile([P, 1], F32, name="zero")
        nc.vector.memset(zero[:], 0.0)
        nc.scalar.activation(out=warm[:], in_=zero[:], func=RELU)
        ident = sb.tile([P, P], F32, name="ident")
        make_identity(nc, ident[:])
        w_plane = sb.tile([P, N], U8, name="w_plane", align_bytes=64)
        nc.vector.memset(w_plane[:].bitcast(I32), 0)

        x_view = xT.rearrange("(p u e) c -> p u e c", u=2, e=2)
        raw = {}

        def load_x(u, c):
            lo, hi = CUTS[u][c], CUTS[u][c + 1]
            raw[u, c] = sb.tile([P, 2, hi - lo], F32, name=f"raw{u}{c}")
            nc.sync.dma_start(out=raw[u, c][:], in_=x_view[:, u, :, lo:hi])

        load_x(0, 0)
        load_x(0, 1)
        nc.sync.dma_start(offsets[:], offs)
        nc.sync.dma_start(out=rows[0:4, :], in_=gate.rearrange("d p v -> (d p) v")[0 : D * P : GATE_ROW_STEP, :])
        nc.sync.dma_start(out=rows[4:6, :], in_=b.rearrange("(r c) o -> r (c o)", r=2))
        load_x(1, 0)
        load_x(1, 1)
        w_codes = sb.tile([P, N], I32, name="w_codes", align_bytes=64)
        nc.sync.dma_start(out=w_codes[:], in_=w_words[0].rearrange("p n t -> p (n t)").bitcast(I32))
        for q in range(4):
            nc.sync.dma_start(
                out=w_plane[32 * q : 32 * q + 4, :].bitcast(I32), in_=w_scales[0, 4 * q : 4 * q + 4, :].bitcast(I32)
            )

        window = [sb.tile([P, T, 2], BF16, name=f"window{u}") for u in range(2)]

        def pair_up(copy, u, c, lo, hi):
            base = CUTS[u][c]
            copy(out=window[u][:, lo:hi, :], in_=raw[u, c][:, :, lo - base : hi - base].rearrange("p e c -> p c e"))

        pair_up(nc.vector.tensor_copy, 0, 0, 0, CUTS[0][1])
        pair_up(nc.vector.tensor_copy, 0, 1, CUTS[0][1], T - SCALAR_SHARE)
        pair_up(nc.scalar.copy, 0, 1, T - SCALAR_SHARE, T)

        def bank(i, slots, name):
            return ps.tile([P, slots, P], F32, name=name, tag=f"bank{i}")

        cols_ps = bank(0, 2, "cols_ps")
        for h in range(2):
            nc.tensor.transpose(cols_ps[:, h, :], rows[:, h * HALF : (h + 1) * HALF], ident[:])
        cols = sb.tile([P, 2, 8], F32, name="cols")
        nc.scalar.copy(out=cols[:], in_=cols_ps[:, :, 0:8])

        def gpsimd_copy(out, in_):
            nc.gpsimd.tensor_scalar(out=out, in0=in_, scalar1=1.0, scalar2=0.0, op0=MULT, op1=ADD)

        pair_up(nc.scalar.copy, 1, 0, CUTS[1][0], CUTS[1][1])
        pair_up(nc.scalar.copy, 1, 1, CUTS[1][1], T - GPSIMD_SHARE)
        pair_up(gpsimd_copy, 1, 1, T - GPSIMD_SHARE, T)

        turned = {}

        def place(i, u, d, halves):
            tile = bank(i, len(halves), f"turned{u}{d}{halves[0]}")
            for slot, h in enumerate(halves):
                turned[u, h, d] = tile[:, slot, :]

        def weight(h, d):
            return cols[:, h, GATE_COL[d] : GATE_COL[d] + 1]

        def gather(u, d, halves, banks):
            if len(banks) == 1:
                place(banks[0], u, d, halves)
            else:
                for h in halves:
                    place(banks[h], u, d, (h,))
            n = HALF * len(halves)
            start = (d * V + halves[0] * HALF) // LIST_COL
            picked = sb.tile([P, 2 * n], BF16, name=f"picked{u}{d}{halves[0]}")
            nc.vector.tensor_copy(
                out=picked[:].bitcast(U32),
                in_=window[u][:].rearrange("p c e -> p (c e)").bitcast(U32).indirect(offsets[:, start : start + n // LIST_COL]),
            )
            for i, h in enumerate(halves):
                nc.tensor.transpose(turned[u, h, d], picked[:].bitcast(F32)[:, i * HALF : (i + 1) * HALF], ident[:])

        grouped = [sb.tile([P, 4 * HALF], BF16, name=f"grouped{h}", align_bytes=64) for h in range(2)]

        term = {}
        part = {}
        x_rows = [sb.tile([P, 2, 2 * P], BF16, name=f"x_rows{h}") for h in range(2)]
        back_ps = {}

        def weigh(u, h, d):
            term[u, h, d] = sb.tile([P, 2 * P], F32, name=f"term{u}{h}{d}")
            nc.scalar.activation(out=term[u, h, d][:], in_=turned[u, h, d].bitcast(BF16), func=COPY, scale=weight(h, d))

        def add_two(u, h):
            part[u, h] = sb.tile([P, 2 * P], F32, name=f"part{u}{h}")
            nc.gpsimd.tensor_tensor(out=part[u, h][:], in0=term[u, h, 0][:], in1=term[u, h, 1][:], op=ADD)

        def add_second(u, h):
            part[u, h] = sb.tile([P, 2 * P], F32, name=f"part{u}{h}")
            nc.vector.scalar_tensor_tensor(
                out=part[u, h][:], in0=turned[u, h, 1].bitcast(BF16), scalar=weight(h, 1), in1=term[u, h, 0][:], op0=MULT, op1=ADD
            )

        def add_last(u, h):
            nc.vector.scalar_tensor_tensor(
                out=x_rows[h][:, u, :], in0=turned[u, h, 2].bitcast(BF16), scalar=weight(h, 2), in1=part[u, h][:], op0=MULT, op1=ADD
            )
            if u == 0:
                back_ps[h] = bank((6, 7)[h], 2, f"back_ps{h}")
            nc.tensor.transpose(back_ps[h][:, u, :], x_rows[h][:, u, :].bitcast(F32), ident[:])

        def interleave(h, copy):
            copy(out=grouped[h][:].bitcast(F32).rearrange("p (v u) -> p v u", u=2), in_=back_ps[h][:].rearrange("p u v -> p v u"))

        acc = {}

        def product(h, banks):
            codes = sb.tile([P, HALF], U32, name=f"codes{h}", align_bytes=64)
            plane = sb.tile([P, HALF], U8, name=f"plane{h}", align_bytes=64)
            nc.vector.quantize_mx(out=codes[:].bitcast(FP8X4), scales=plane[:], in_=grouped[h][:])
            per_bank = 4 // len(banks)
            tiles = [bank(i, per_bank, f"acc{h}{i}") for i in banks]
            for j in range(4):
                acc[h, j] = tiles[j // per_bank][:, j % per_bank, :]
                m = slice(j * P, (j + 1) * P)
                nc.tensor.matmul_mx(
                    out=acc[h, j],
                    lhsT=w_codes[:, m].bitcast(FP8X4),
                    lhsT_scale=w_plane[:, m],
                    rhs=codes[:].bitcast(FP8X4),
                    rhs_scale=plane[:],
                    start=True,
                    stop=True,
                )

        out_view = out.rearrange("(j p) v -> p j v", p=P)

        def finish(h, js, on_vector):
            res = sb.tile([P, len(js), HALF], F32, name=f"res{h}{js[0]}")
            for i, j in enumerate(js):
                bias = cols[:, j % 2, BIAS_COL + j // 2 : BIAS_COL + j // 2 + 1]
                if on_vector[i]:
                    nc.vector.tensor_scalar(out=res[:, i, :], in0=acc[h, j], scalar1=bias, scalar2=0.0, op0=ADD, op1=MAX)
                else:
                    nc.scalar.activation(out=res[:, i, :], in_=acc[h, j], func=RELU, bias=bias)
            nc.sync.dma_start(out=out_view[:, js[0] : js[-1] + 1, h * HALF : (h + 1) * HALF], in_=res[:])

        gather(0, 0, (0, 1), (1,))
        gather(0, 1, (0, 1), (2,))
        gather(0, 2, (0, 1), (3,))
        for h in range(2):
            weigh(0, h, 0)
            weigh(0, h, 1)
            add_two(0, h)
        gather(1, 0, (0, 1), (4,))
        gather(1, 1, (0,), (0,))
        gather(1, 2, (0,), (2,))
        gather(1, 1, (1,), (5,))
        weigh(1, 0, 0)
        weigh(1, 1, 0)
        add_second(1, 0)
        add_last(0, 0)
        add_last(1, 0)
        gather(1, 2, (1,), (1,))
        add_second(1, 1)
        add_last(0, 1)
        interleave(0, nc.scalar.copy)
        add_last(1, 1)
        interleave(1, nc.scalar.copy)
        product(0, (4, 0, 2, 6))
        product(1, (1, 3, 5, 7))
        finish(0, (0, 1), (True, False))
        finish(0, (2, 3), (True, False))
        finish(1, (0, 1), (False, True))
        finish(1, (2, 3), (False, True))
